import numpy as np
import ml_dtypes


def mxq(x, axis, fmt="e4m3"):
    dtype, down = {"e4m3": (ml_dtypes.float8_e4m3fn, 7), "e5m2": (ml_dtypes.float8_e5m2, 14)}[fmt]
    v = np.moveaxis(np.asarray(x, np.float32).astype(ml_dtypes.bfloat16).astype(np.float64), axis, -1)
    blocks = v.reshape(v.shape[:-1] + (-1, 32))
    amax = np.abs(blocks).max(-1, keepdims=True)
    byte = np.maximum(np.where(amax > 0, np.frexp(amax)[1] - 1 + 127, 0) - down, 1)
    scale = np.exp2(byte - 127.0)
    codes = (blocks / scale).astype(np.float32).astype(dtype).astype(np.float64)
    return np.moveaxis((codes * scale).reshape(v.shape), -1, axis)


WIDE = False


def mx_kscale(k):
    if not WIDE:
        return np.ones(k)
    levels = np.array([10, -10, 5, -5, 0])
    if k % 512:
        return np.exp2(np.random.permutation(np.resize(levels, k // 32))).repeat(32)
    a = np.empty((k // 512, 16))
    for p in range(k // 512):
        a[p, :8] = np.random.permutation(np.resize(levels, 8))
        for g in range(8):
            far = levels[np.abs(levels - a[p, g]) >= 10]
            a[p, g + 8] = far[np.random.randint(len(far))]
    return np.exp2(a.ravel()).repeat(32)


def f64(x):
    return np.asarray(x).astype(np.float64)


def striped(idx):
    return np.tile(idx.reshape(-1, 16).T, (8, 1)).astype(np.uint16)


def unstriped(offs):
    return offs[:16].T.reshape(-1).astype(np.int64)


def silu(v):
    return v / (1.0 + np.exp(-np.maximum(v, -700.0)))


K, T, E, C, H, N = 1024, 512, 4, 256, 512, 512


def by_expert(wq, xq):
    return np.concatenate([wq[e].T @ xq[:, e * C:(e + 1) * C] for e in range(E)], axis=1)


def setup_inputs():
    n = np.random.standard_normal
    s = mx_kscale(K)[:, None]
    u = mx_kscale(H)
    first = np.random.permutation(np.repeat(np.arange(E), T // E))
    second = (first + 1 + np.random.permutation(np.repeat(np.arange(E - 1), -(-T // (E - 1)))[:T])) % E
    while np.bincount(second, minlength=E).max() != T // E:
        load = np.bincount(second, minlength=E); hi, lo = int(load.argmax()), int(load.argmin())
        t = np.flatnonzero((second == hi) & (first != lo))[0]; second[t] = lo
    slot_token = np.empty(E * C, np.int64); pos = np.empty((2, T), np.int64); fill = np.zeros(E, np.int64)
    place = np.stack([np.random.permutation(C) for _ in range(E)])
    for r, deal in enumerate((first, second)):
        for t in np.random.permutation(T):
            e = deal[t]; j = e * C + place[e, fill[e]]; fill[e] += 1; slot_token[j] = t; pos[r, t] = j
    g = np.random.uniform(0.2, 0.8, T)
    return {
        "xT": (n((K, T)) * s).astype(np.float32),
        "w1": (n((E, K, H)) / np.sqrt(K) / s[None]).astype(np.float32),
        "w3": (n((E, K, H)) / np.sqrt(K) / s[None] * u[None, None, :]).astype(np.float32),
        "w2": (n((E, H, N)) / np.sqrt(H) / u[None, :, None]).astype(np.float32),
        "gate": np.stack([np.tile(g, (N, 1)), np.tile(1.0 - g, (N, 1))]).astype(np.float32),
        "offs": striped(slot_token),
        "pos1": striped(pos[0]),
        "pos2": striped(pos[1]),
    }


def reference(xT, w1, w3, w2, gate, offs, pos1, pos2):
    idx = unstriped(offs)
    xq = mxq(f64(xT)[:, idx], 0, "e4m3")
    h = silu(by_expert(mxq(f64(w1), 1, "e4m3"), xq))
    h = h * by_expert(mxq(f64(w3), 1, "e4m3"), xq)
    y = by_expert(mxq(f64(w2), 1, "e4m3"), mxq(h, 0, "e4m3"))
    return f64(gate[0]) * y[:, unstriped(pos1)] + f64(gate[1]) * y[:, unstriped(pos2)]

@@ -1,0 +1,189 @@
+from contextlib import ExitStack
+
+import concourse.mybir as mybir
+
+K, T, E, C, H, N = 1024, 512, 4, 256, 512, 512
+FLOPS = 2 * E * C * (2 * K * H + H * N)
+
+F32 = mybir.dt.float32
+BF16 = mybir.dt.bfloat16
+U32 = mybir.dt.uint32
+U16 = mybir.dt.uint16
+U8 = mybir.dt.uint8
+FP8X4 = mybir.dt.float8_e4m3fn_x4
+MULT = mybir.AluOpType.mult
+ADD = mybir.AluOpType.add
+COPY = mybir.ActivationFunctionType.Copy
+SILU = mybir.ActivationFunctionType.Silu
+
+P = 128
+PASSES = K // 512
+HALF = 128
+X_CUT = 160
+W_CUT = 24
+
+
+def tile_routed_moe_kernel(tc, xT, w1, w3, w2, gate, offs, pos1, pos2, out):
+    nc = tc.nc
+    with ExitStack() as ctx:
+        keep = ctx.enter_context(tc.tile_pool(name="keep", bufs=1))
+        raws = ctx.enter_context(tc.tile_pool(name="raws", bufs=11))
+        laids = ctx.enter_context(tc.tile_pool(name="laids", bufs=5))
+        work = ctx.enter_context(tc.tile_pool(name="work", bufs=2))
+        small = ctx.enter_context(tc.tile_pool(name="small", bufs=2))
+        wcodes = ctx.enter_context(tc.tile_pool(name="wcodes", bufs=10))
+        banks_a = ctx.enter_context(tc.psum_pool(name="banks_a", bufs=3))
+        banks_b = ctx.enter_context(tc.psum_pool(name="banks_b", bufs=3))
+        banks_y = ctx.enter_context(tc.psum_pool(name="banks_y", bufs=2))
+
+        spark = keep.tile([P, 1], F32, name="spark")
+        nc.vector.memset(spark[:], 0.0)
+        nc.scalar.activation(spark[:], spark[:], SILU)
+
+        offs_sb = keep.tile([P, E * C // 16], U16, name="offs_sb")
+        pos_sb = [keep.tile([P, T // 16], U16, name="pos1_sb"), keep.tile([P, T // 16], U16, name="pos2_sb")]
+
+        nc.sync.dma_start(offs_sb[:], offs)
+        x_words = []
+        x_scales = keep.tile([P, T], U8, name="x_scales", align_bytes=64)
+        x_raw = []
+        for g in range(PASSES):
+            for q in range(2):
+                raw = raws.tile([P, 4, T // 2], F32, name="raw")
+                nc.sync.dma_start(raw[:], xT[g * 512 : (g + 1) * 512, q * 256 : (q + 1) * 256].rearrange("(p j) n -> p j n", j=4))
+                x_raw.append(raw)
+        for g in range(PASSES):
+            words = keep.tile([P, T], U32, name="xw%d" % g, align_bytes=64)
+            x_words.append(words)
+            for q in range(2):
+                raw = x_raw[2 * g + q]
+                laid = laids.tile([P, 1024], BF16, name="laid", align_bytes=64)
+                dst = laid[:].rearrange("p (n j) -> p n j", j=4)
+                src = raw[:].rearrange("p j n -> p n j")
+                nc.vector.tensor_copy(dst[:, 0:X_CUT, :], src[:, 0:X_CUT, :])
+                nc.scalar.copy(dst[:, X_CUT:256, :], src[:, X_CUT:256, :])
+                cols = slice(q * 256, (q + 1) * 256)
+                nc.vector.quantize_mx(out=words[:, cols].bitcast(FP8X4), scales=x_scales[4 * g : P, cols], in_=laid[:])
+
+        nc.sync.dma_start(pos_sb[0][:], pos1)
+        nc.sync.dma_start(pos_sb[1][:], pos2)
+
+        def gather_tokens(e):
+            lst = offs_sb[:, e * C // 16 : (e + 1) * C // 16]
+            gs = keep.tile([P, C], U8, name="gs%d" % e, align_bytes=64)
+            nc.vector.tensor_copy(gs[:], x_scales[:].indirect(lst))
+            got = []
+            for g in range(PASSES):
+                gw = keep.tile([P, C], U32, name="gw%d_%d" % (e, g), align_bytes=64)
+                nc.vector.tensor_copy(gw[:], x_words[g][:].indirect(lst))
+                got.append((gw, gs[4 * g : P, :]))
+            return got
+
+        def quantise_weights(w, e, g):
+            raw = raws.tile([P, 4, H], F32, name="raw")
+            nc.sync.dma_start(raw[:], w[e, g * 512 : (g + 1) * 512, :].rearrange("(p j) i -> p j i", j=4))
+            laid = laids.tile([P, 2048], BF16, name="laid", align_bytes=64)
+            dst = laid[:].rearrange("p (t m j) -> p m t j", t=4, j=4)
+            src = raw[:].rearrange("p j (m t) -> p m t j", t=4)
+            nc.vector.tensor_copy(dst[:, 0:W_CUT], src[:, 0:W_CUT])
+            nc.scalar.copy(dst[:, W_CUT:128], src[:, W_CUT:128])
+            ww = wcodes.tile([P, H], U32, name="ww", align_bytes=64)
+            ws = wcodes.tile([P, H], U8, name="ws", align_bytes=64)
+            nc.vector.quantize_mx(out=ww[:].bitcast(FP8X4), scales=ws[:], in_=laid[:])
+            return ww, ws, laid
+
+        def product(got, codes, pool, name, cols):
+            bank = pool.tile([P, 4, HALF], F32, name=name)
+            for t in range(4):
+                for g in range(PASSES):
+                    ww, ws = codes[g][:2]
+                    gw, gs = got[g]
+                    nc.tensor.matmul_mx(
+                        out=bank[:, t, :],
+                        lhsT=ww[:, t * P : (t + 1) * P].bitcast(FP8X4),
+                        lhsT_scale=ws[:, t * P : (t + 1) * P],
+                        rhs=gw[:, cols].bitcast(FP8X4),
+                        rhs_scale=gs[:, cols],
+                        start=(g == 0),
+                        stop=(g == PASSES - 1),
+                    )
+            return bank
+
+        h_words, h_scales = [], []
+
+        def hidden(pairs, behind):
+            hw = keep.tile([P, C], U32, name="hw%d" % len(h_words), align_bytes=64)
+            hs = keep.tile([P, C], U8, name="hs%d" % len(h_words), align_bytes=64)
+            zero = small.tile([P, 1], F32, name="zero")
+            nc.scalar.activation(zero[:], behind[:, 4 * W_CUT : 4 * W_CUT + 1], COPY, scale=0.0)
+            for half, (bank1, bank3) in enumerate(pairs):
+                cols = slice(half * HALF, (half + 1) * HALF)
+                act = work.tile([P, 4, HALF], F32, name="act")
+                nc.scalar.activation(act[:], bank1[:], SILU, bias=zero[:])
+                hid = work.tile([P, HALF * 4], BF16, name="hid", align_bytes=64)
+                nc.vector.tensor_tensor(
+                    hid[:].rearrange("p (n t) -> p n t", t=4),
+                    bank3[:].rearrange("p t n -> p n t"),
+                    act[:].rearrange("p t n -> p n t"),
+                    MULT,
+                )
+                nc.vector.quantize_mx(out=hw[:, cols].bitcast(FP8X4), scales=hs[:, cols], in_=hid[:])
+            h_words.append(hw)
+            h_scales.append(hs)
+
+        pairs = None
+        for e in range(E):
+            got = gather_tokens(e)
+            codes1 = [quantise_weights(w1, e, g) for g in range(PASSES)]
+            if e > 0:
+                hidden(pairs, codes1[1][2])
+            codes3 = [quantise_weights(w3, e, g) for g in range(PASSES)]
+            pairs = []
+            for half in range(2):
+                cols = slice(half * HALF, (half + 1) * HALF)
+                pairs.append((product(got, codes1, banks_a, "bank_a", cols), product(got, codes3, banks_b, "bank_b", cols)))
+        hidden(pairs, codes3[1][2])
+
+        raw2, gates = [], []
+        for b in range(N // P + 1):
+            if b < N // P:
+                raw = raws.tile([P, E, 4, P], F32, name="raw")
+                for e in range(E):
+                    nc.sync.dma_start(raw[:, e], w2[e, :, b * P : (b + 1) * P].rearrange("(p j) n -> p j n", j=4))
+                raw2.append(raw)
+            if b > 0:
+                gt = keep.tile([P, 2, T], F32, name="gates%d" % b)
+                nc.sync.dma_start(gt[:], gate[:, (b - 1) * P : b * P, :].rearrange("r p n -> p r n"))
+                gates.append(gt)
+        for b in range(N // P):
+            laid = laids.tile([P, 2048], BF16, name="laid", align_bytes=64)
+            dst = laid[:].rearrange("p (e n j) -> p e n j", e=E, j=4)
+            src = raw2[b][:].rearrange("p e j n -> p e n j")
+            nc.scalar.copy(dst[:, 0:2], src[:, 0:2])
+            nc.scalar.copy(dst[:, 2:4], src[:, 2:4])
+            ww = keep.tile([P, E * P], U32, name="w2w%d" % b, align_bytes=64)
+            ws = keep.tile([P, E * P], U8, name="w2s%d" % b, align_bytes=64)
+            nc.vector.quantize_mx(out=ww[:].bitcast(FP8X4), scales=ws[:], in_=laid[:])
+            y = keep.tile([P, E * C], F32, name="y%d" % b)
+            for two in range(2):
+                bank = banks_y.tile([P, 2, C], F32, name="bank_y")
+                for k in range(2):
+                    e = 2 * two + k
+                    nc.tensor.matmul_mx(
+                        out=bank[:, k, :],
+                        lhsT=ww[:, e * P : (e + 1) * P].bitcast(FP8X4),
+                        lhsT_scale=ws[:, e * P : (e + 1) * P],
+                        rhs=h_words[e][:].bitcast(FP8X4),
+                        rhs_scale=h_scales[e][:],
+                        start=True,
+                        stop=True,
+                    )
+                nc.scalar.copy(y[:, two * 2 * C : (two + 1) * 2 * C], bank[:].rearrange("p k n -> p (k n)"))
+            parts = []
+            for r in range(2):
+                part = work.tile([P, T], F32, name="part%d" % r)
+                nc.vector.tensor_tensor(part[:], y[:].indirect(pos_sb[r][:]), gates[b][:, r, :], MULT)
+                parts.append(part)
+            total = work.tile([P, T], F32, name="total")
+            nc.vector.tensor_tensor(total[:], parts[0][:], parts[1][:], ADD)
+            nc.sync.dma_start(out[b * P : (b + 1) * P, :], total[:])

@@ -19,8 +19,8 @@ SILU = mybir.ActivationFunctionType.Silu
 P = 128
 PASSES = K // 512
 HALF = 128
-X_CUT = 160
-W_CUT = 24
+X_CUT = 40
+W_CUT = 36
 
 
 def tile_routed_moe_kernel(tc, xT, w1, w3, w2, gate, offs, pos1, pos2, out):
@@ -58,10 +58,10 @@ def tile_routed_moe_kernel(tc, xT, w1, w3, w2, gate, offs, pos1, pos2, out):
             for q in range(2):
                 raw = x_raw[2 * g + q]
                 laid = laids.tile([P, 1024], BF16, name="laid", align_bytes=64)
-                dst = laid[:].rearrange("p (n j) -> p n j", j=4)
-                src = raw[:].rearrange("p j n -> p n j")
-                nc.vector.tensor_copy(dst[:, 0:X_CUT, :], src[:, 0:X_CUT, :])
-                nc.scalar.copy(dst[:, X_CUT:256, :], src[:, X_CUT:256, :])
+                dst = laid[:].rearrange("p (c i j) -> p c j i", i=4, j=4)
+                src = raw[:].rearrange("p j (c i) -> p c j i", i=4)
+                nc.vector.tensor_copy(dst[:, 0:X_CUT], src[:, 0:X_CUT])
+                nc.scalar.copy(dst[:, X_CUT:64], src[:, X_CUT:64])
                 cols = slice(q * 256, (q + 1) * 256)
                 nc.vector.quantize_mx(out=words[:, cols].bitcast(FP8X4), scales=x_scales[4 * g : P, cols], in_=laid[:])
 
@@ -83,8 +83,8 @@ def tile_routed_moe_kernel(tc, xT, w1, w3, w2, gate, offs, pos1, pos2, out):
             raw = raws.tile([P, 4, H], F32, name="raw")
             nc.sync.dma_start(raw[:], w[e, g * 512 : (g + 1) * 512, :].rearrange("(p j) i -> p j i", j=4))
             laid = laids.tile([P, 2048], BF16, name="laid", align_bytes=64)
-            dst = laid[:].rearrange("p (t m j) -> p m t j", t=4, j=4)
-            src = raw[:].rearrange("p j (m t) -> p m t j", t=4)
+            dst = laid[:].rearrange("p (t m j) -> p m j t", t=4, j=4)
+            src = raw[:].rearrange("p j (m t) -> p m j t", t=4)
             nc.vector.tensor_copy(dst[:, 0:W_CUT], src[:, 0:W_CUT])
             nc.scalar.copy(dst[:, W_CUT:128], src[:, W_CUT:128])
             ww = wcodes.tile([P, H], U32, name="ww", align_bytes=64)
@@ -144,23 +144,34 @@ def tile_routed_moe_kernel(tc, xT, w1, w3, w2, gate, offs, pos1, pos2, out):
                 pairs.append((product(got, codes1, banks_a, "bank_a", cols), product(got, codes3, banks_b, "bank_b", cols)))
         hidden(pairs, codes3[1][2])
 
-        raw2, gates = [], []
-        for b in range(N // P + 1):
-            if b < N // P:
+        pieces = {}
+        gates = None
+        for blocks in ((0,), (1,), (2, 3)):
+            width = len(blocks) * P
+            lo = blocks[0] * P
+            if width == P:
                 raw = raws.tile([P, E, 4, P], F32, name="raw")
                 for e in range(E):
-                    nc.sync.dma_start(raw[:, e], w2[e, :, b * P : (b + 1) * P].rearrange("(p j) n -> p j n", j=4))
-                raw2.append(raw)
-            if b > 0:
-                gt = keep.tile([P, 2, T], F32, name="gates%d" % b)
-                nc.sync.dma_start(gt[:], gate[:, (b - 1) * P : b * P, :].rearrange("r p n -> p r n"))
-                gates.append(gt)
+                    nc.sync.dma_start(raw[:, e], w2[e, :, lo : lo + P].rearrange("(p j) n -> p j n", j=4))
+                pieces[blocks[0]] = [raw[:, 0:2], raw[:, 2:4]]
+            else:
+                halves = []
+                for two in range(2):
+                    raw = raws.tile([P, 2, 4, width], F32, name="raw")
+                    for k in range(2):
+                        nc.sync.dma_start(raw[:, k], w2[2 * two + k, :, lo : lo + width].rearrange("(p j) n -> p j n", j=4))
+                    halves.append(raw)
+                for s, b in enumerate(blocks):
+                    pieces[b] = [raw[:, :, :, s * P : (s + 1) * P] for raw in halves]
+            if gates is None:
+                gates = keep.tile([P, 2, T], F32, name="gates")
+                nc.sync.dma_start(gates[:], gate[:, 0:P, :].rearrange("r p n -> p r n"))
         for b in range(N // P):
             laid = laids.tile([P, 2048], BF16, name="laid", align_bytes=64)
-            dst = laid[:].rearrange("p (e n j) -> p e n j", e=E, j=4)
-            src = raw2[b][:].rearrange("p e j n -> p e n j")
-            nc.scalar.copy(dst[:, 0:2], src[:, 0:2])
-            nc.scalar.copy(dst[:, 2:4], src[:, 2:4])
+            dst = laid[:].rearrange("p (e c i j) -> p e c j i", e=E, i=4, j=4)
+            for two in range(2):
+                src = pieces[b][two].rearrange("p e j (c i) -> p e c j i", i=4)
+                nc.scalar.copy(dst[:, 2 * two : 2 * two + 2], src)
             ww = keep.tile([P, E * P], U32, name="w2w%d" % b, align_bytes=64)
             ws = keep.tile([P, E * P], U8, name="w2s%d" % b, align_bytes=64)
             nc.vector.quantize_mx(out=ww[:].bitcast(FP8X4), scales=ws[:], in_=laid[:])
@@ -182,7 +193,7 @@ def tile_routed_moe_kernel(tc, xT, w1, w3, w2, gate, offs, pos1, pos2, out):
             parts = []
             for r in range(2):
                 part = work.tile([P, T], F32, name="part%d" % r)
-                nc.vector.tensor_tensor(part[:], y[:].indirect(pos_sb[r][:]), gates[b][:, r, :], MULT)
+                nc.vector.tensor_tensor(part[:], y[:].indirect(pos_sb[r][:]), gates[:, r, :], MULT)
                 parts.append(part)
             total = work.tile([P, T], F32, name="total")
             nc.vector.tensor_tensor(total[:], parts[0][:], parts[1][:], ADD)

@@ -20,7 +20,7 @@ P = 128
 PASSES = K // 512
 HALF = 128
 X_CUT = 40
-W_CUT = 36
+W_CUT = 52
 
 
 def tile_routed_moe_kernel(tc, xT, w1, w3, w2, gate, offs, pos1, pos2, out):
@@ -79,14 +79,19 @@ def tile_routed_moe_kernel(tc, xT, w1, w3, w2, gate, offs, pos1, pos2, out):
                 got.append((gw, gs[4 * g : P, :]))
             return got
 
-        def quantise_weights(w, e, g):
+        def quantise_weights(w, e, g, parts=1, cut=W_CUT):
             raw = raws.tile([P, 4, H], F32, name="raw")
-            nc.sync.dma_start(raw[:], w[e, g * 512 : (g + 1) * 512, :].rearrange("(p j) i -> p j i", j=4))
+            rows = w[e, g * 512 : (g + 1) * 512, :].rearrange("(p j) i -> p j i", j=4)
+            for part in range(parts):
+                cols = slice(part * H // parts, (part + 1) * H // parts)
+                nc.sync.dma_start(raw[:, :, cols], rows[:, :, cols])
             laid = laids.tile([P, 2048], BF16, name="laid", align_bytes=64)
             dst = laid[:].rearrange("p (t m j) -> p m j t", t=4, j=4)
             src = raw[:].rearrange("p j (m t) -> p m j t", t=4)
-            nc.vector.tensor_copy(dst[:, 0:W_CUT], src[:, 0:W_CUT])
-            nc.scalar.copy(dst[:, W_CUT:128], src[:, W_CUT:128])
+            for part in range(parts):
+                lo, mid, hi = part * 128 // parts, part * 128 // parts + cut, (part + 1) * 128 // parts
+                nc.vector.tensor_copy(dst[:, lo:mid], src[:, lo:mid])
+                nc.scalar.copy(dst[:, mid:hi], src[:, mid:hi])
             ww = wcodes.tile([P, H], U32, name="ww", align_bytes=64)
             ws = wcodes.tile([P, H], U8, name="ws", align_bytes=64)
             nc.vector.quantize_mx(out=ww[:].bitcast(FP8X4), scales=ws[:], in_=laid[:])
@@ -115,7 +120,7 @@ def tile_routed_moe_kernel(tc, xT, w1, w3, w2, gate, offs, pos1, pos2, out):
             hw = keep.tile([P, C], U32, name="hw%d" % len(h_words), align_bytes=64)
             hs = keep.tile([P, C], U8, name="hs%d" % len(h_words), align_bytes=64)
             zero = small.tile([P, 1], F32, name="zero")
-            nc.scalar.activation(zero[:], behind[:, 4 * W_CUT : 4 * W_CUT + 1], COPY, scale=0.0)
+            nc.scalar.activation(zero[:], behind[:, 508:509], COPY, scale=0.0)
             for half, (bank1, bank3) in enumerate(pairs):
                 cols = slice(half * HALF, (half + 1) * HALF)
                 act = work.tile([P, 4, HALF], F32, name="act")
@@ -137,7 +142,7 @@ def tile_routed_moe_kernel(tc, xT, w1, w3, w2, gate, offs, pos1, pos2, out):
             codes1 = [quantise_weights(w1, e, g) for g in range(PASSES)]
             if e > 0:
                 hidden(pairs, codes1[1][2])
-            codes3 = [quantise_weights(w3, e, g) for g in range(PASSES)]
+            codes3 = [quantise_weights(w3, e, g, *((2, 32) if e == E - 1 else ())) for g in range(PASSES)]
             pairs = []
             for half in range(2):
                 cols = slice(half * HALF, (half + 1) * HALF)
@@ -166,15 +171,26 @@ def tile_routed_moe_kernel(tc, xT, w1, w3, w2, gate, offs, pos1, pos2, out):
             if gates is None:
                 gates = keep.tile([P, 2, T], F32, name="gates")
                 nc.sync.dma_start(gates[:], gate[:, 0:P, :].rearrange("r p n -> p r n"))
-        for b in range(N // P):
-            laid = laids.tile([P, 2048], BF16, name="laid", align_bytes=64)
-            dst = laid[:].rearrange("p (e c i j) -> p e c j i", e=E, i=4, j=4)
-            for two in range(2):
-                src = pieces[b][two].rearrange("p e j (c i) -> p e c j i", i=4)
-                nc.scalar.copy(dst[:, 2 * two : 2 * two + 2], src)
+        laid2 = {}
+
+        def interleave_half(b, two):
+            if b not in laid2:
+                laid = laids.tile([P, 2048], BF16, name="laid", align_bytes=64)
+                laid2[b] = laid
+            dst = laid2[b][:].rearrange("p (e c i j) -> p e c j i", e=E, i=4, j=4)
+            src = pieces[b][two].rearrange("p e j (c i) -> p e c j i", i=4)
+            nc.scalar.copy(dst[:, 2 * two : 2 * two + 2], src)
+
+        codes2 = []
+
+        def quantise2(b):
             ww = keep.tile([P, E * P], U32, name="w2w%d" % b, align_bytes=64)
             ws = keep.tile([P, E * P], U8, name="w2s%d" % b, align_bytes=64)
-            nc.vector.quantize_mx(out=ww[:].bitcast(FP8X4), scales=ws[:], in_=laid[:])
+            nc.vector.quantize_mx(out=ww[:].bitcast(FP8X4), scales=ws[:], in_=laid2[b][:])
+            codes2.append((ww, ws))
+
+        def slots(b):
+            ww, ws = codes2[b]
             y = keep.tile([P, E * C], F32, name="y%d" % b)
             for two in range(2):
                 bank = banks_y.tile([P, 2, C], F32, name="bank_y")
@@ -189,12 +205,38 @@ def tile_routed_moe_kernel(tc, xT, w1, w3, w2, gate, offs, pos1, pos2, out):
                         start=True,
                         stop=True,
                     )
-                nc.scalar.copy(y[:, two * 2 * C : (two + 1) * 2 * C], bank[:].rearrange("p k n -> p (k n)"))
-            parts = []
-            for r in range(2):
-                part = work.tile([P, T], F32, name="part%d" % r)
-                nc.vector.tensor_tensor(part[:], y[:].indirect(pos_sb[r][:]), gates[:, r, :], MULT)
-                parts.append(part)
-            total = work.tile([P, T], F32, name="total")
-            nc.vector.tensor_tensor(total[:], parts[0][:], parts[1][:], ADD)
+                dst = y[:, two * 2 * C : (two + 1) * 2 * C]
+                src = bank[:].rearrange("p k n -> p (k n)")
+                if b == 0 and two == 1:
+                    nc.vector.tensor_copy(dst, src)
+                else:
+                    nc.scalar.copy(dst, src)
+            return y
+
+        parts = {}
+
+        def fetch(b, r, y):
+            part = work.tile([P, T], F32, name="part%d" % r)
+            nc.vector.tensor_tensor(part[:], y[:].indirect(pos_sb[r][:]), gates[:, r, :], MULT)
+            parts[b, r] = part
+
+        def finish(b):
+            total = keep.tile([P, T], F32, name="total%d" % b)
+            nc.vector.tensor_tensor(total[:], parts[b, 0][:], parts[b, 1][:], ADD)
             nc.sync.dma_start(out[b * P : (b + 1) * P, :], total[:])
+
+        last = N // P - 1
+        interleave_half(0, 0)
+        interleave_half(0, 1)
+        quantise2(0)
+        for b in range(N // P):
+            y = slots(b)
+            if b < last:
+                interleave_half(b + 1, 0)
+                interleave_half(b + 1, 1)
+                quantise2(b + 1)
+            fetch(b, 0, y)
+            if b > 0:
+                finish(b - 1)
+            fetch(b, 1, y)
+        finish(last)

@@ -19,7 +19,7 @@ SILU = mybir.ActivationFunctionType.Silu
 P = 128
 PASSES = K // 512
 HALF = 128
-X_CUT = 40
+X_CUT = 80
 W_CUT = 52
 
 
@@ -48,22 +48,18 @@ def tile_routed_moe_kernel(tc, xT, w1, w3, w2, gate, offs, pos1, pos2, out):
         x_scales = keep.tile([P, T], U8, name="x_scales", align_bytes=64)
         x_raw = []
         for g in range(PASSES):
-            for q in range(2):
-                raw = raws.tile([P, 4, T // 2], F32, name="raw")
-                nc.sync.dma_start(raw[:], xT[g * 512 : (g + 1) * 512, q * 256 : (q + 1) * 256].rearrange("(p j) n -> p j n", j=4))
-                x_raw.append(raw)
+            raw = raws.tile([P, 4, T], F32, name="raw")
+            nc.sync.dma_start(raw[:], xT[g * 512 : (g + 1) * 512, :].rearrange("(p j) n -> p j n", j=4))
+            x_raw.append(raw)
         for g in range(PASSES):
             words = keep.tile([P, T], U32, name="xw%d" % g, align_bytes=64)
             x_words.append(words)
-            for q in range(2):
-                raw = x_raw[2 * g + q]
-                laid = laids.tile([P, 1024], BF16, name="laid", align_bytes=64)
-                dst = laid[:].rearrange("p (c i j) -> p c j i", i=4, j=4)
-                src = raw[:].rearrange("p j (c i) -> p c j i", i=4)
-                nc.vector.tensor_copy(dst[:, 0:X_CUT], src[:, 0:X_CUT])
-                nc.scalar.copy(dst[:, X_CUT:64], src[:, X_CUT:64])
-                cols = slice(q * 256, (q + 1) * 256)
-                nc.vector.quantize_mx(out=words[:, cols].bitcast(FP8X4), scales=x_scales[4 * g : P, cols], in_=laid[:])
+            laid = laids.tile([P, 2048], BF16, name="laid", align_bytes=64)
+            dst = laid[:].rearrange("p (c i j) -> p c j i", i=4, j=4)
+            src = x_raw[g][:].rearrange("p j (c i) -> p c j i", i=4)
+            nc.vector.tensor_copy(dst[:, 0:X_CUT], src[:, 0:X_CUT])
+            nc.scalar.copy(dst[:, X_CUT:128], src[:, X_CUT:128])
+            nc.vector.quantize_mx(out=words[:].bitcast(FP8X4), scales=x_scales[4 * g : P, :], in_=laid[:])
 
         nc.sync.dma_start(pos_sb[0][:], pos1)
         nc.sync.dma_start(pos_sb[1][:], pos2)
@@ -79,19 +75,15 @@ def tile_routed_moe_kernel(tc, xT, w1, w3, w2, gate, offs, pos1, pos2, out):
                 got.append((gw, gs[4 * g : P, :]))
             return got
 
-        def quantise_weights(w, e, g, parts=1, cut=W_CUT):
+        def quantise_weights(w, e, g, cut=W_CUT):
             raw = raws.tile([P, 4, H], F32, name="raw")
             rows = w[e, g * 512 : (g + 1) * 512, :].rearrange("(p j) i -> p j i", j=4)
-            for part in range(parts):
-                cols = slice(part * H // parts, (part + 1) * H // parts)
-                nc.sync.dma_start(raw[:, :, cols], rows[:, :, cols])
+            nc.sync.dma_start(raw[:], rows)
             laid = laids.tile([P, 2048], BF16, name="laid", align_bytes=64)
             dst = laid[:].rearrange("p (t m j) -> p m j t", t=4, j=4)
             src = raw[:].rearrange("p j (m t) -> p m j t", t=4)
-            for part in range(parts):
-                lo, mid, hi = part * 128 // parts, part * 128 // parts + cut, (part + 1) * 128 // parts
-                nc.vector.tensor_copy(dst[:, lo:mid], src[:, lo:mid])
-                nc.scalar.copy(dst[:, mid:hi], src[:, mid:hi])
+            nc.vector.tensor_copy(dst[:, 0:cut], src[:, 0:cut])
+            nc.scalar.copy(dst[:, cut:128], src[:, cut:128])
             ww = wcodes.tile([P, H], U32, name="ww", align_bytes=64)
             ws = wcodes.tile([P, H], U8, name="ws", align_bytes=64)
             nc.vector.quantize_mx(out=ww[:].bitcast(FP8X4), scales=ws[:], in_=laid[:])
@@ -119,12 +111,15 @@ def tile_routed_moe_kernel(tc, xT, w1, w3, w2, gate, offs, pos1, pos2, out):
         def hidden(pairs, behind):
             hw = keep.tile([P, C], U32, name="hw%d" % len(h_words), align_bytes=64)
             hs = keep.tile([P, C], U8, name="hs%d" % len(h_words), align_bytes=64)
-            zero = small.tile([P, 1], F32, name="zero")
-            nc.scalar.activation(zero[:], behind[:, 508:509], COPY, scale=0.0)
+            bias = 0.0
+            if behind is not None:
+                zero = small.tile([P, 1], F32, name="zero")
+                nc.scalar.activation(zero[:], behind[:, 508:509], COPY, scale=0.0)
+                bias = zero[:]
             for half, (bank1, bank3) in enumerate(pairs):
                 cols = slice(half * HALF, (half + 1) * HALF)
                 act = work.tile([P, 4, HALF], F32, name="act")
-                nc.scalar.activation(act[:], bank1[:], SILU, bias=zero[:])
+                nc.scalar.activation(act[:], bank1[:], SILU, bias=bias)
                 hid = work.tile([P, HALF * 4], BF16, name="hid", align_bytes=64)
                 nc.vector.tensor_tensor(
                     hid[:].rearrange("p (n t) -> p n t", t=4),
@@ -142,34 +137,24 @@ def tile_routed_moe_kernel(tc, xT, w1, w3, w2, gate, offs, pos1, pos2, out):
             codes1 = [quantise_weights(w1, e, g) for g in range(PASSES)]
             if e > 0:
                 hidden(pairs, codes1[1][2])
-            codes3 = [quantise_weights(w3, e, g, *((2, 32) if e == E - 1 else ())) for g in range(PASSES)]
+            codes3 = [quantise_weights(w3, e, g, 72 if (e, g) == (E - 1, PASSES - 1) else W_CUT) for g in range(PASSES)]
             pairs = []
             for half in range(2):
                 cols = slice(half * HALF, (half + 1) * HALF)
                 pairs.append((product(got, codes1, banks_a, "bank_a", cols), product(got, codes3, banks_b, "bank_b", cols)))
-        hidden(pairs, codes3[1][2])
+        hidden(pairs, None)
 
         pieces = {}
-        gates = None
-        for blocks in ((0,), (1,), (2, 3)):
-            width = len(blocks) * P
-            lo = blocks[0] * P
-            if width == P:
-                raw = raws.tile([P, E, 4, P], F32, name="raw")
-                for e in range(E):
-                    nc.sync.dma_start(raw[:, e], w2[e, :, lo : lo + P].rearrange("(p j) n -> p j n", j=4))
-                pieces[blocks[0]] = [raw[:, 0:2], raw[:, 2:4]]
-            else:
-                halves = []
-                for two in range(2):
-                    raw = raws.tile([P, 2, 4, width], F32, name="raw")
-                    for k in range(2):
-                        nc.sync.dma_start(raw[:, k], w2[2 * two + k, :, lo : lo + width].rearrange("(p j) n -> p j n", j=4))
-                    halves.append(raw)
-                for s, b in enumerate(blocks):
-                    pieces[b] = [raw[:, :, :, s * P : (s + 1) * P] for raw in halves]
-            if gates is None:
-                gates = keep.tile([P, 2, T], F32, name="gates")
+        gates = keep.tile([P, 2, T], F32, name="gates")
+        for side in range(2):
+            lo = side * 2 * P
+            for two in range(2):
+                raw = raws.tile([P, 2, 4, 2 * P], F32, name="raw")
+                for k in range(2):
+                    nc.sync.dma_start(raw[:, k], w2[2 * two + k, :, lo : lo + 2 * P].rearrange("(p j) n -> p j n", j=4))
+                for s in range(2):
+                    pieces[2 * side + s, two] = raw[:, :, :, s * P : (s + 1) * P]
+            if side == 0:
                 nc.sync.dma_start(gates[:], gate[:, 0:P, :].rearrange("r p n -> p r n"))
         laid2 = {}
 
@@ -178,8 +163,11 @@ def tile_routed_moe_kernel(tc, xT, w1, w3, w2, gate, offs, pos1, pos2, out):
                 laid = laids.tile([P, 2048], BF16, name="laid", align_bytes=64)
                 laid2[b] = laid
             dst = laid2[b][:].rearrange("p (e c i j) -> p e c j i", e=E, i=4, j=4)
-            src = pieces[b][two].rearrange("p e j (c i) -> p e c j i", i=4)
-            nc.scalar.copy(dst[:, 2 * two : 2 * two + 2], src)
+            src = pieces[b, two].rearrange("p e j (c i) -> p e c j i", i=4)
+            if (b, two) == (0, 1):
+                nc.vector.tensor_copy(dst[:, 2 * two : 2 * two + 2], src)
+            else:
+                nc.scalar.copy(dst[:, 2 * two : 2 * two + 2], src)
 
         codes2 = []
 

@@ -1,6 +1,7 @@
 from contextlib import ExitStack
 
 import concourse.mybir as mybir
+from concourse.masks import make_identity
 
 K, T, E, C, H, N = 1024, 512, 4, 256, 512, 512
 FLOPS = 2 * E * C * (2 * K * H + H * N)
@@ -20,7 +21,6 @@ P = 128
 PASSES = K // 512
 HALF = 128
 X_CUT = 80
-W_CUT = 52
 
 
 def tile_routed_moe_kernel(tc, xT, w1, w3, w2, gate, offs, pos1, pos2, out):
@@ -32,9 +32,13 @@ def tile_routed_moe_kernel(tc, xT, w1, w3, w2, gate, offs, pos1, pos2, out):
         work = ctx.enter_context(tc.tile_pool(name="work", bufs=2))
         small = ctx.enter_context(tc.tile_pool(name="small", bufs=2))
         wcodes = ctx.enter_context(tc.tile_pool(name="wcodes", bufs=10))
-        banks_a = ctx.enter_context(tc.psum_pool(name="banks_a", bufs=3))
-        banks_b = ctx.enter_context(tc.psum_pool(name="banks_b", bufs=3))
+        banks_a = ctx.enter_context(tc.psum_pool(name="banks_a", bufs=2))
+        banks_b = ctx.enter_context(tc.psum_pool(name="banks_b", bufs=2))
         banks_y = ctx.enter_context(tc.psum_pool(name="banks_y", bufs=2))
+
+        banks_sum = ctx.enter_context(tc.psum_pool(name="banks_sum", bufs=2))
+        ident = keep.tile([P, P], F32, name="ident")
+        make_identity(nc, ident[:])
 
         spark = keep.tile([P, 1], F32, name="spark")
         nc.vector.memset(spark[:], 0.0)
@@ -75,15 +79,17 @@ def tile_routed_moe_kernel(tc, xT, w1, w3, w2, gate, offs, pos1, pos2, out):
                 got.append((gw, gs[4 * g : P, :]))
             return got
 
-        def quantise_weights(w, e, g, cut=W_CUT):
+        def quantise_weights(w, e, g, cut):
             raw = raws.tile([P, 4, H], F32, name="raw")
             rows = w[e, g * 512 : (g + 1) * 512, :].rearrange("(p j) i -> p j i", j=4)
             nc.sync.dma_start(raw[:], rows)
             laid = laids.tile([P, 2048], BF16, name="laid", align_bytes=64)
             dst = laid[:].rearrange("p (t m j) -> p m j t", t=4, j=4)
             src = raw[:].rearrange("p j (m t) -> p m j t", t=4)
-            nc.vector.tensor_copy(dst[:, 0:cut], src[:, 0:cut])
-            nc.scalar.copy(dst[:, cut:128], src[:, cut:128])
+            if cut > 0:
+                nc.vector.tensor_copy(dst[:, 0:cut], src[:, 0:cut])
+            if cut < 128:
+                nc.scalar.copy(dst[:, cut:128], src[:, cut:128])
             ww = wcodes.tile([P, H], U32, name="ww", align_bytes=64)
             ws = wcodes.tile([P, H], U8, name="ws", align_bytes=64)
             nc.vector.quantize_mx(out=ww[:].bitcast(FP8X4), scales=ws[:], in_=laid[:])
@@ -116,28 +122,32 @@ def tile_routed_moe_kernel(tc, xT, w1, w3, w2, gate, offs, pos1, pos2, out):
                 zero = small.tile([P, 1], F32, name="zero")
                 nc.scalar.activation(zero[:], behind[:, 508:509], COPY, scale=0.0)
                 bias = zero[:]
+            hid = work.tile([P, C * 4], BF16, name="hid", align_bytes=64)
             for half, (bank1, bank3) in enumerate(pairs):
                 cols = slice(half * HALF, (half + 1) * HALF)
                 act = work.tile([P, 4, HALF], F32, name="act")
                 nc.scalar.activation(act[:], bank1[:], SILU, bias=bias)
-                hid = work.tile([P, HALF * 4], BF16, name="hid", align_bytes=64)
+                words = slice(half * HALF * 4, (half + 1) * HALF * 4)
                 nc.vector.tensor_tensor(
-                    hid[:].rearrange("p (n t) -> p n t", t=4),
+                    hid[:, words].rearrange("p (n t) -> p n t", t=4),
                     bank3[:].rearrange("p t n -> p n t"),
                     act[:].rearrange("p t n -> p n t"),
                     MULT,
                 )
-                nc.vector.quantize_mx(out=hw[:, cols].bitcast(FP8X4), scales=hs[:, cols], in_=hid[:])
+                if len(h_words) == E - 1:
+                    nc.vector.quantize_mx(out=hw[:, cols].bitcast(FP8X4), scales=hs[:, cols], in_=hid[:, words])
+            if len(h_words) < E - 1:
+                nc.vector.quantize_mx(out=hw[:].bitcast(FP8X4), scales=hs[:], in_=hid[:])
             h_words.append(hw)
             h_scales.append(hs)
 
         pairs = None
         for e in range(E):
             got = gather_tokens(e)
-            codes1 = [quantise_weights(w1, e, g) for g in range(PASSES)]
+            codes1 = [quantise_weights(w1, e, g, (0, 64)[g]) for g in range(PASSES)]
             if e > 0:
                 hidden(pairs, codes1[1][2])
-            codes3 = [quantise_weights(w3, e, g, 72 if (e, g) == (E - 1, PASSES - 1) else W_CUT) for g in range(PASSES)]
+            codes3 = [quantise_weights(w3, e, g, ((128, 0), (64, 72))[e == E - 1][g]) for g in range(PASSES)]
             pairs = []
             for half in range(2):
                 cols = slice(half * HALF, (half + 1) * HALF)
@@ -164,10 +174,7 @@ def tile_routed_moe_kernel(tc, xT, w1, w3, w2, gate, offs, pos1, pos2, out):
                 laid2[b] = laid
             dst = laid2[b][:].rearrange("p (e c i j) -> p e c j i", e=E, i=4, j=4)
             src = pieces[b, two].rearrange("p e j (c i) -> p e c j i", i=4)
-            if (b, two) == (0, 1):
-                nc.vector.tensor_copy(dst[:, 2 * two : 2 * two + 2], src)
-            else:
-                nc.scalar.copy(dst[:, 2 * two : 2 * two + 2], src)
+            nc.scalar.copy(dst[:, 2 * two : 2 * two + 2], src)
 
         codes2 = []
 
@@ -210,19 +217,29 @@ def tile_routed_moe_kernel(tc, xT, w1, w3, w2, gate, offs, pos1, pos2, out):
 
         def finish(b):
             total = keep.tile([P, T], F32, name="total%d" % b)
-            nc.vector.tensor_tensor(total[:], parts[b, 0][:], parts[b, 1][:], ADD)
+            if b < 2:
+                bank = banks_sum.tile([P, T], F32, name="bank_sum")
+                for r in range(2):
+                    nc.tensor.matmul(bank[:], ident[:], parts[b, r][:], start=(r == 0), stop=(r == 1))
+                nc.scalar.copy(total[:], bank[:])
+            else:
+                nc.vector.tensor_tensor(total[:], parts[b, 0][:], parts[b, 1][:], ADD)
             nc.sync.dma_start(out[b * P : (b + 1) * P, :], total[:])
 
         last = N // P - 1
-        interleave_half(0, 0)
-        interleave_half(0, 1)
-        quantise2(0)
+        ys = []
+        for b in range(2):
+            interleave_half(b, 0)
+            interleave_half(b, 1)
+            quantise2(b)
+            ys.append(slots(b))
         for b in range(N // P):
-            y = slots(b)
-            if b < last:
-                interleave_half(b + 1, 0)
-                interleave_half(b + 1, 1)
-                quantise2(b + 1)
+            y = ys[b]
+            if b < last - 1:
+                interleave_half(b + 2, 0)
+                interleave_half(b + 2, 1)
+                quantise2(b + 2)
+                ys.append(slots(b + 2))
             fetch(b, 0, y)
             if b > 0:
                 finish(b - 1)

from contextlib import ExitStack

import concourse.mybir as mybir
from concourse.masks import make_identity

K, T, E, C, H, N = 1024, 512, 4, 256, 512, 512
FLOPS = 2 * E * C * (2 * K * H + H * N)

F32 = mybir.dt.float32
BF16 = mybir.dt.bfloat16
U32 = mybir.dt.uint32
U16 = mybir.dt.uint16
U8 = mybir.dt.uint8
FP8X4 = mybir.dt.float8_e4m3fn_x4
MULT = mybir.AluOpType.mult
ADD = mybir.AluOpType.add
COPY = mybir.ActivationFunctionType.Copy
SILU = mybir.ActivationFunctionType.Silu

P = 128
PASSES = K // 512
HALF = 128
X_CUT = 80


def tile_routed_moe_kernel(tc, xT, w1, w3, w2, gate, offs, pos1, pos2, out):
    nc = tc.nc
    with ExitStack() as ctx:
        keep = ctx.enter_context(tc.tile_pool(name="keep", bufs=1))
        raws = ctx.enter_context(tc.tile_pool(name="raws", bufs=11))
        laids = ctx.enter_context(tc.tile_pool(name="laids", bufs=5))
        work = ctx.enter_context(tc.tile_pool(name="work", bufs=2))
        small = ctx.enter_context(tc.tile_pool(name="small", bufs=2))
        wcodes = ctx.enter_context(tc.tile_pool(name="wcodes", bufs=10))
        banks_a = ctx.enter_context(tc.psum_pool(name="banks_a", bufs=2))
        banks_b = ctx.enter_context(tc.psum_pool(name="banks_b", bufs=2))
        banks_y = ctx.enter_context(tc.psum_pool(name="banks_y", bufs=2))

        banks_sum = ctx.enter_context(tc.psum_pool(name="banks_sum", bufs=2))
        ident = keep.tile([P, P], F32, name="ident")
        make_identity(nc, ident[:])

        spark = keep.tile([P, 1], F32, name="spark")
        nc.vector.memset(spark[:], 0.0)
        nc.scalar.activation(spark[:], spark[:], SILU)

        offs_sb = keep.tile([P, E * C // 16], U16, name="offs_sb")
        pos_sb = [keep.tile([P, T // 16], U16, name="pos1_sb"), keep.tile([P, T // 16], U16, name="pos2_sb")]

        nc.sync.dma_start(offs_sb[:], offs)
        x_words = []
        x_scales = keep.tile([P, T], U8, name="x_scales", align_bytes=64)
        x_raw = []
        for g in range(PASSES):
            raw = raws.tile([P, 4, T], F32, name="raw")
            nc.sync.dma_start(raw[:], xT[g * 512 : (g + 1) * 512, :].rearrange("(p j) n -> p j n", j=4))
            x_raw.append(raw)
        for g in range(PASSES):
            words = keep.tile([P, T], U32, name="xw%d" % g, align_bytes=64)
            x_words.append(words)
            laid = laids.tile([P, 2048], BF16, name="laid", align_bytes=64)
            dst = laid[:].rearrange("p (c i j) -> p c j i", i=4, j=4)
            src = x_raw[g][:].rearrange("p j (c i) -> p c j i", i=4)
            nc.vector.tensor_copy(dst[:, 0:X_CUT], src[:, 0:X_CUT])
            nc.scalar.copy(dst[:, X_CUT:128], src[:, X_CUT:128])
            nc.vector.quantize_mx(out=words[:].bitcast(FP8X4), scales=x_scales[4 * g : P, :], in_=laid[:])

        nc.sync.dma_start(pos_sb[0][:], pos1)
        nc.sync.dma_start(pos_sb[1][:], pos2)

        def gather_tokens(e):
            lst = offs_sb[:, e * C // 16 : (e + 1) * C // 16]
            gs = keep.tile([P, C], U8, name="gs%d" % e, align_bytes=64)
            nc.vector.tensor_copy(gs[:], x_scales[:].indirect(lst))
            got = []
            for g in range(PASSES):
                gw = keep.tile([P, C], U32, name="gw%d_%d" % (e, g), align_bytes=64)
                nc.vector.tensor_copy(gw[:], x_words[g][:].indirect(lst))
                got.append((gw, gs[4 * g : P, :]))
            return got

        def quantise_weights(w, e, g, cut):
            raw = raws.tile([P, 4, H], F32, name="raw")
            rows = w[e, g * 512 : (g + 1) * 512, :].rearrange("(p j) i -> p j i", j=4)
            nc.sync.dma_start(raw[:], rows)
            laid = laids.tile([P, 2048], BF16, name="laid", align_bytes=64)
            dst = laid[:].rearrange("p (t m j) -> p m j t", t=4, j=4)
            src = raw[:].rearrange("p j (m t) -> p m j t", t=4)
            if cut > 0:
                nc.vector.tensor_copy(dst[:, 0:cut], src[:, 0:cut])
            if cut < 128:
                nc.scalar.copy(dst[:, cut:128], src[:, cut:128])
            ww = wcodes.tile([P, H], U32, name="ww", align_bytes=64)
            ws = wcodes.tile([P, H], U8, name="ws", align_bytes=64)
            nc.vector.quantize_mx(out=ww[:].bitcast(FP8X4), scales=ws[:], in_=laid[:])
            return ww, ws, laid

        def product(got, codes, pool, name, cols):
            bank = pool.tile([P, 4, HALF], F32, name=name)
            for t in range(4):
                for g in range(PASSES):
                    ww, ws = codes[g][:2]
                    gw, gs = got[g]
                    nc.tensor.matmul_mx(
                        out=bank[:, t, :],
                        lhsT=ww[:, t * P : (t + 1) * P].bitcast(FP8X4),
                        lhsT_scale=ws[:, t * P : (t + 1) * P],
                        rhs=gw[:, cols].bitcast(FP8X4),
                        rhs_scale=gs[:, cols],
                        start=(g == 0),
                        stop=(g == PASSES - 1),
                    )
            return bank

        h_words, h_scales = [], []

        def hidden(pairs, behind):
            hw = keep.tile([P, C], U32, name="hw%d" % len(h_words), align_bytes=64)
            hs = keep.tile([P, C], U8, name="hs%d" % len(h_words), align_bytes=64)
            bias = 0.0
            if behind is not None:
                zero = small.tile([P, 1], F32, name="zero")
                nc.scalar.activation(zero[:], behind[:, 508:509], COPY, scale=0.0)
                bias = zero[:]
            hid = work.tile([P, C * 4], BF16, name="hid", align_bytes=64)
            for half, (bank1, bank3) in enumerate(pairs):
                cols = slice(half * HALF, (half + 1) * HALF)
                act = work.tile([P, 4, HALF], F32, name="act")
                nc.scalar.activation(act[:], bank1[:], SILU, bias=bias)
                words = slice(half * HALF * 4, (half + 1) * HALF * 4)
                nc.vector.tensor_tensor(
                    hid[:, words].rearrange("p (n t) -> p n t", t=4),
                    bank3[:].rearrange("p t n -> p n t"),
                    act[:].rearrange("p t n -> p n t"),
                    MULT,
                )
                if len(h_words) == E - 1:
                    nc.vector.quantize_mx(out=hw[:, cols].bitcast(FP8X4), scales=hs[:, cols], in_=hid[:, words])
            if len(h_words) < E - 1:
                nc.vector.quantize_mx(out=hw[:].bitcast(FP8X4), scales=hs[:], in_=hid[:])
            h_words.append(hw)
            h_scales.append(hs)

        pairs = None
        for e in range(E):
            got = gather_tokens(e)
            codes1 = [quantise_weights(w1, e, g, (0, 64)[g]) for g in range(PASSES)]
            if e > 0:
                hidden(pairs, codes1[1][2])
            codes3 = [quantise_weights(w3, e, g, ((128, 0), (64, 72))[e == E - 1][g]) for g in range(PASSES)]
            pairs = []
            for half in range(2):
                cols = slice(half * HALF, (half + 1) * HALF)
                pairs.append((product(got, codes1, banks_a, "bank_a", cols), product(got, codes3, banks_b, "bank_b", cols)))
        hidden(pairs, None)

        pieces = {}
        gates = keep.tile([P, 2, T], F32, name="gates")
        for side in range(2):
            lo = side * 2 * P
            for two in range(2):
                raw = raws.tile([P, 2, 4, 2 * P], F32, name="raw")
                for k in range(2):
                    nc.sync.dma_start(raw[:, k], w2[2 * two + k, :, lo : lo + 2 * P].rearrange("(p j) n -> p j n", j=4))
                for s in range(2):
                    pieces[2 * side + s, two] = raw[:, :, :, s * P : (s + 1) * P]
            if side == 0:
                nc.sync.dma_start(gates[:], gate[:, 0:P, :].rearrange("r p n -> p r n"))
        laid2 = {}

        def interleave_half(b, two):
            if b not in laid2:
                laid = laids.tile([P, 2048], BF16, name="laid", align_bytes=64)
                laid2[b] = laid
            dst = laid2[b][:].rearrange("p (e c i j) -> p e c j i", e=E, i=4, j=4)
            src = pieces[b, two].rearrange("p e j (c i) -> p e c j i", i=4)
            nc.scalar.copy(dst[:, 2 * two : 2 * two + 2], src)

        codes2 = []

        def quantise2(b):
            ww = keep.tile([P, E * P], U32, name="w2w%d" % b, align_bytes=64)
            ws = keep.tile([P, E * P], U8, name="w2s%d" % b, align_bytes=64)
            nc.vector.quantize_mx(out=ww[:].bitcast(FP8X4), scales=ws[:], in_=laid2[b][:])
            codes2.append((ww, ws))

        def slots(b):
            ww, ws = codes2[b]
            y = keep.tile([P, E * C], F32, name="y%d" % b)
            for two in range(2):
                bank = banks_y.tile([P, 2, C], F32, name="bank_y")
                for k in range(2):
                    e = 2 * two + k
                    nc.tensor.matmul_mx(
                        out=bank[:, k, :],
                        lhsT=ww[:, e * P : (e + 1) * P].bitcast(FP8X4),
                        lhsT_scale=ws[:, e * P : (e + 1) * P],
                        rhs=h_words[e][:].bitcast(FP8X4),
                        rhs_scale=h_scales[e][:],
                        start=True,
                        stop=True,
                    )
                dst = y[:, two * 2 * C : (two + 1) * 2 * C]
                src = bank[:].rearrange("p k n -> p (k n)")
                if b == 0 and two == 1:
                    nc.vector.tensor_copy(dst, src)
                else:
                    nc.scalar.copy(dst, src)
            return y

        parts = {}

        def fetch(b, r, y):
            part = work.tile([P, T], F32, name="part%d" % r)
            nc.vector.tensor_tensor(part[:], y[:].indirect(pos_sb[r][:]), gates[:, r, :], MULT)
            parts[b, r] = part

        def finish(b):
            total = keep.tile([P, T], F32, name="total%d" % b)
            if b < 2:
                bank = banks_sum.tile([P, T], F32, name="bank_sum")
                for r in range(2):
                    nc.tensor.matmul(bank[:], ident[:], parts[b, r][:], start=(r == 0), stop=(r == 1))
                nc.scalar.copy(total[:], bank[:])
            else:
                nc.vector.tensor_tensor(total[:], parts[b, 0][:], parts[b, 1][:], ADD)
            nc.sync.dma_start(out[b * P : (b + 1) * P, :], total[:])

        last = N // P - 1
        ys = []
        for b in range(2):
            interleave_half(b, 0)
            interleave_half(b, 1)
            quantise2(b)
            ys.append(slots(b))
        for b in range(N // P):
            y = ys[b]
            if b < last - 1:
                interleave_half(b + 2, 0)
                interleave_half(b + 2, 1)
                quantise2(b + 2)
                ys.append(slots(b + 2))
            fetch(b, 0, y)
            if b > 0:
                finish(b - 1)
            fetch(b, 1, y)
        finish(last)
